import numpy as np
import ml_dtypes


def mxq(x, axis, fmt="e4m3"):
    dtype, down = {"e4m3": (ml_dtypes.float8_e4m3fn, 7), "e5m2": (ml_dtypes.float8_e5m2, 14)}[fmt]
    v = np.moveaxis(np.asarray(x, np.float32).astype(ml_dtypes.bfloat16).astype(np.float64), axis, -1)
    blocks = v.reshape(v.shape[:-1] + (-1, 32))
    amax = np.abs(blocks).max(-1, keepdims=True)
    byte = np.maximum(np.where(amax > 0, np.frexp(amax)[1] - 1 + 127, 0) - down, 1)
    scale = np.exp2(byte - 127.0)
    codes = (blocks / scale).astype(np.float32).astype(dtype).astype(np.float64)
    return np.moveaxis((codes * scale).reshape(v.shape), -1, axis)


WIDE = False


def mx_kscale(k):
    if not WIDE:
        return np.ones(k)
    levels = np.array([10, -10, 5, -5, 0])
    if k % 512:
        return np.exp2(np.random.permutation(np.resize(levels, k // 32))).repeat(32)
    a = np.empty((k // 512, 16))
    for p in range(k // 512):
        a[p, :8] = np.random.permutation(np.resize(levels, 8))
        for g in range(8):
            far = levels[np.abs(levels - a[p, g]) >= 10]
            a[p, g + 8] = far[np.random.randint(len(far))]
    return np.exp2(a.ravel()).repeat(32)


def f64(x):
    return np.asarray(x).astype(np.float64)


def striped(idx):
    return np.tile(idx.reshape(-1, 16).T, (8, 1)).astype(np.uint16)


def unstriped(offs):
    return offs[:16].T.reshape(-1).astype(np.int64)


def striped8(idx):
    return np.concatenate([x.reshape(-1, 16).T for x in idx]).astype(np.uint16)


def runs(offs, k):
    lists = np.stack([offs[16 * r : 16 * r + 16].T.reshape(-1) for r in range(8)]).astype(np.int64)
    return lists[np.arange(k) % 512 // 64]


def pack_weight(w):
    k, n = w.shape
    w = f64(np.asarray(w, np.float32).astype(ml_dtypes.bfloat16)).reshape(k // 32, 32, n)
    amax = np.abs(w).max(1)
    byte = np.clip(np.where(amax > 0, np.frexp(amax)[1] - 1 + 127 - 7, 1), 1, 254)
    scaled = (w * np.exp2(127.0 - byte)[:, None, :]).reshape(k, n).astype(np.float32)
    words = np.ascontiguousarray(scaled.reshape(k // 512, 128, 4, n).transpose(0, 1, 3, 2)).astype(ml_dtypes.float8_e4m3fn).view(np.uint8)
    return words, np.ascontiguousarray(byte.astype(np.uint8).reshape(k // 512, 16, n))


def unpack_weight(words, scales):
    g, p, n, _ = words.shape
    vals = np.ascontiguousarray(words).view(ml_dtypes.float8_e4m3fn).astype(np.float64) * np.repeat(np.exp2(scales.astype(np.float64) - 127.0), 8, axis=1)[..., None]
    return vals.transpose(0, 1, 3, 2).reshape(g * 512, n)


K, T, S, H, W = 512, 2048, 512, 512, 256


def setup_inputs():
    n = np.random.standard_normal
    s = mx_kscale(K)[:, None]
    u = mx_kscale(S)
    packed_xT = pack_weight(n((K, T)) * s)
    perm = np.stack([np.random.permutation(S) for _ in range(8)])
    return {
        "x_words": packed_xT[0],
        "x_scales": packed_xT[1],
        "w1": (n((K, H)) / np.sqrt(K) / s).astype(np.float32),
        "ga": (np.random.uniform(0.5, 1.5, (H, 1)) * u[:, None]).astype(np.float32),
        "gb": (np.random.uniform(0.5, 1.5, (H, 1)) / u[:, None]).astype(np.float32),
        "offs": striped(np.random.permutation(T)[:S]),
        "n1": striped8(perm[:, :W]),
        "n2": striped8(perm[:, W:]),
        "n3": striped(np.random.permutation(S)),
        "n4": striped(np.random.permutation(S)),
        "n5": striped(np.random.permutation(S)),
        "n6": striped8(np.stack([np.random.permutation(S) for _ in range(8)])),
    }


def reference(x_words, x_scales, w1, ga, gb, offs, n1, n2, n3, n4, n5, n6):
    xq = unpack_weight(x_words, x_scales)[:, unstriped(offs)]
    y = mxq(f64(w1), 0, "e4m3").T @ xq
    pa = y[np.arange(H)[:, None], runs(n1, H)]
    pb = y[np.arange(H)[:, None], runs(n2, H)]
    ra = np.maximum(pa, pb)
    ds = y.copy()
    ds[np.arange(H)[:, None], runs(n1, H)] = ra
    z = f64(ga) * ds
    ex = np.exp(0.5 * y)
    z2 = f64(gb) * (np.log((ex + ex[:, unstriped(n3)]) / (ex[:, unstriped(n4)] + ex[:, unstriped(n5)])))
    s = 0.0625 * ((mxq(z, 0, "e4m3").T @ mxq(z2, 0, "e4m3")))
    pa2 = s[np.arange(S)[:, None], runs(n6, S)]
    return (2.0 * (s * pa2)) / ((s) ** 2 + (pa2) ** 2 + 0.5)

@@ -1,0 +1,229 @@
+from contextlib import ExitStack
+
+import concourse.mybir as mybir
+from concourse.masks import make_identity
+
+K, T, S, H, W = 512, 2048, 512, 512, 256
+FLOPS = 2 * K * H * S + 2 * H * S * S
+
+F32 = mybir.dt.float32
+BF16 = mybir.dt.bfloat16
+I32 = mybir.dt.int32
+U32 = mybir.dt.uint32
+U16 = mybir.dt.uint16
+U8 = mybir.dt.uint8
+FP8X4 = mybir.dt.float8_e4m3fn_x4
+ACT = mybir.ActivationFunctionType
+ALU = mybir.AluOpType
+
+P = 128
+PACK = 4
+CHUNK = 256
+
+
+def tile_picked_selffilloddsharm_none_p_kernel(
+    tc, x_words, x_scales, w1, ga, gb, offs, n1, n2, n3, n4, n5, n6, out
+):
+    nc = tc.nc
+    with ExitStack() as ctx:
+        lists = ctx.enter_context(tc.tile_pool(name="lists", bufs=1))
+        keep = ctx.enter_context(tc.tile_pool(name="keep", bufs=1))
+        ring = ctx.enter_context(tc.tile_pool(name="ring", bufs=2))
+        psum = ctx.enter_context(tc.psum_pool(name="psum", bufs=1))
+
+        def load_list(name, source):
+            tile = lists.tile([P, source.shape[1]], U16, name=name)
+            nc.sync.dma_start(tile[:], source)
+            return tile
+
+        table_scales = keep.tile([P, T], U8, name="table_scales")
+        nc.gpsimd.memset(table_scales[:].bitcast(I32), 0)
+        offs_sb = load_list("offs_sb", offs)
+        w_rows = w1.rearrange("(p j) c -> p j c", j=PACK)
+        w_raw = [keep.tile([P, PACK, H // 2], F32, name="w_raw%d" % h) for h in range(2)]
+        nc.sync.dma_start(w_raw[0][:], w_rows[:, :, : H // 2])
+        for q in range(4):
+            nc.sync.dma_start(
+                table_scales[32 * q : 32 * q + 4, :].bitcast(I32), x_scales[0, 4 * q : 4 * q + 4, :].bitcast(I32)
+            )
+        nc.sync.dma_start(w_raw[1][:], w_rows[:, :, H // 2 :])
+        table_words = keep.tile([P, T], U32, name="table_words")
+        nc.sync.dma_start(table_words[:].bitcast(I32), x_words[0].rearrange("p n t -> p (n t)").bitcast(I32))
+        n2_sb = load_list("n2_sb", n2)
+        n1_sb = load_list("n1_sb", n1)
+        n4_sb = load_list("n4_sb", n4)
+        n5_sb = load_list("n5_sb", n5)
+        n3_sb = load_list("n3_sb", n3)
+        ga_sb = keep.tile([P, PACK], F32, name="ga_sb")
+        nc.sync.dma_start(ga_sb[:], ga.rearrange("(p t) o -> p (t o)", t=PACK))
+        gb_sb = keep.tile([P, PACK], F32, name="gb_sb")
+        nc.sync.dma_start(gb_sb[:], gb.rearrange("(p t) o -> p (t o)", t=PACK))
+        n6_sb = load_list("n6_sb", n6)
+        ident = keep.tile([P, P], F32, name="ident")
+        make_identity(nc, ident[:])
+
+        w_bf = keep.tile([P, PACK, P, PACK], BF16, name="w_bf", align_bytes=64)
+        for h in range(2):
+            nc.scalar.activation(
+                w_bf[:, :, h * 64 : (h + 1) * 64, :].rearrange("p t m j -> p m j t"),
+                w_raw[h][:].rearrange("p j (m t) -> p m j t", t=PACK),
+                ACT.Copy,
+            )
+        x_sc = keep.tile([P, S], U8, name="x_sc", align_bytes=64)
+        nc.vector.tensor_copy(x_sc[:], table_scales[:].indirect(offs_sb[:]))
+        w_codes = keep.tile([P, H], U32, name="w_codes", align_bytes=64)
+        w_sc = keep.tile([P, H], U8, name="w_sc", align_bytes=64)
+        nc.vector.quantize_mx(
+            out=w_codes[:].bitcast(FP8X4), scales=w_sc[:], in_=w_bf[:].rearrange("p t m j -> p (t m j)")
+        )
+        x_codes = keep.tile([P, S], U32, name="x_codes", align_bytes=64)
+        for h in range(2):
+            nc.vector.tensor_copy(
+                x_codes[:, h * W : (h + 1) * W], table_words[:].indirect(offs_sb[:, h * 16 : (h + 1) * 16])
+            )
+
+        ex = [keep.tile([P, S], F32, name="ex%d" % t) for t in range(PACK)]
+        y = [keep.tile([P, S], F32, name="y%d" % t) for t in range(PACK)]
+        pieces = [(0, 0, W), (1, 0, W), (0, W, S), (1, W, S), (2, 0, S), (3, 0, S)]
+        for bank, (t, lo, hi) in enumerate(pieces):
+            y_ps = psum.tile([P, hi - lo], F32, name="y_ps", tag="bank%d" % bank)
+            cols = slice(t * P, (t + 1) * P)
+            nc.tensor.matmul_mx(
+                out=y_ps[:],
+                lhsT=w_codes[:, cols].bitcast(FP8X4),
+                lhsT_scale=w_sc[:, cols],
+                rhs=x_codes[:, lo:hi].bitcast(FP8X4),
+                rhs_scale=x_sc[:, lo:hi],
+                start=True,
+                stop=True,
+            )
+            nc.scalar.activation(ex[t][:, lo:hi], y_ps[:], ACT.Exp, scale=0.5)
+            nc.vector.tensor_copy(y[t][:, lo:hi], y_ps[:])
+
+        z_planes = keep.tile([P, PACK, S], BF16, name="z_planes")
+        for t in range(PACK):
+            pb = ring.tile([P, W], F32, name="pb", bufs=4)
+            nc.scalar.activation(pb[:], y[t][:].indirect(n2_sb[:]), ACT.Copy)
+            pa = ring.tile([P, W], F32, name="pa", bufs=4)
+            nc.vector.tensor_copy(pa[:], y[t][:].indirect(n1_sb[:]))
+            ra = ring.tile([P, W], F32, name="ra")
+            nc.vector.tensor_tensor(ra[:], pa[:], pb[:], ALU.max)
+            nc.vector.tensor_copy(y[t][:].indirect(n1_sb[:]), ra[:])
+            nc.vector.tensor_scalar(z_planes[:, t, :], y[t][:], ga_sb[:, t : t + 1], None, ALU.mult)
+        z_bf = keep.tile([P, PACK, P, PACK], BF16, name="z_bf", align_bytes=64)
+        z_codes = keep.tile([P, S], U32, name="z_codes", align_bytes=64)
+        z_sc = keep.tile([P, S], U8, name="z_sc", align_bytes=64)
+        nc.vector.tensor_copy(
+            z_bf[:].rearrange("p t m j -> p m j t"), z_planes[:].rearrange("p j (m t) -> p m j t", t=PACK)
+        )
+        nc.vector.quantize_mx(
+            out=z_codes[:].bitcast(FP8X4), scales=z_sc[:], in_=z_bf[:].rearrange("p t m j -> p (t m j)")
+        )
+
+        s_win = [keep.tile([P, 2 * S], F32, name="s_win%d" % t) for t in range(PACK)]
+        for t in range(PACK):
+            nc.gpsimd.memset(s_win[t][:, S:], 0.0)
+        s_sq = [keep.tile([P, S], F32, name="s_sq%d" % t) for t in range(PACK)]
+        blocks = CHUNK // P
+
+        def turn(bank, t, source, start, stop):
+            nc.tensor.matmul(bank[:, t, :], lhsT=source, rhs=ident[:], start=start, stop=stop, is_transpose=True)
+
+        for c in range(S // CHUNK):
+            entries = slice(c * CHUNK // 16, (c + 1) * CHUNK // 16)
+            den = [psum.tile([P, PACK, P], F32, name="den", tag="bank%d" % (4 + b)) for b in range(blocks)]
+            num = [psum.tile([P, PACK, P], F32, name="num", tag="bank%d" % (6 + b)) for b in range(blocks)]
+            for t in range(PACK):
+                e4 = ring.tile([P, CHUNK], F32, name="e4", bufs=4)
+                nc.scalar.activation(e4[:], ex[t][:].indirect(n4_sb[:, entries]), ACT.Copy)
+                e5 = ring.tile([P, CHUNK], F32, name="e5", bufs=4)
+                nc.scalar.activation(e5[:], ex[t][:].indirect(n5_sb[:, entries]), ACT.Copy)
+                for b in range(blocks):
+                    turn(den[b], t, e4[:, b * P : (b + 1) * P], True, False)
+                for b in range(blocks):
+                    turn(den[b], t, e5[:, b * P : (b + 1) * P], False, True)
+            for b in range(blocks):
+                first = c * CHUNK + b * P
+                for t in range(PACK):
+                    turn(num[b], t, ex[t][:, first : first + P], t == 0, False)
+            for t in range(PACK):
+                e3 = ring.tile([P, CHUNK], F32, name="e3", bufs=4)
+                nc.scalar.activation(e3[:], ex[t][:].indirect(n3_sb[:, entries]), ACT.Copy)
+                for b in range(blocks):
+                    turn(num[b], t, e3[:, b * P : (b + 1) * P], False, t == PACK - 1)
+            back = [psum.tile([P, PACK, P], F32, name="back", tag="bank%d" % b) for b in range(blocks)]
+            for b in range(blocks):
+                ln_den = ring.tile([P, PACK, P], F32, name="ln_den")
+                nc.scalar.activation(ln_den[:], den[b][:], ACT.Ln)
+                minus = ring.tile([P, PACK, P], F32, name="minus")
+                nc.vector.tensor_scalar(minus[:], ln_den[:], -1.0, None, ALU.mult)
+                for t in range(PACK):
+                    turn(back[b], t, minus[:, t, :], t == 0, False)
+            z2_codes = ring.tile([P, CHUNK], U32, name="z2_codes", align_bytes=64)
+            z2_sc = ring.tile([P, CHUNK], U8, name="z2_sc", align_bytes=64)
+            for b in range(blocks):
+                ln_num = ring.tile([P, PACK, P], F32, name="ln_num")
+                nc.scalar.activation(ln_num[:], num[b][:], ACT.Ln)
+                for t in range(PACK):
+                    turn(back[b], t, ln_num[:, t, :], False, t == PACK - 1)
+                z2_bf = ring.tile([P, P, PACK], BF16, name="z2_bf", align_bytes=64)
+                nc.vector.tensor_tensor(
+                    z2_bf[:],
+                    back[b][:].rearrange("p t j -> p j t"),
+                    gb_sb[:].unsqueeze(1).to_broadcast([P, P, PACK]),
+                    ALU.mult,
+                )
+                nc.vector.quantize_mx(
+                    out=z2_codes[:, b * P : (b + 1) * P].bitcast(FP8X4),
+                    scales=z2_sc[:, b * P : (b + 1) * P],
+                    in_=z2_bf[:].rearrange("p j t -> p (j t)"),
+                )
+            places = slice(c * CHUNK, (c + 1) * CHUNK)
+            for t in range(PACK):
+                s_ps = psum.tile([P, CHUNK], F32, name="s_ps", tag="bank%d" % (2 + t % 2))
+                cols = slice(t * P, (t + 1) * P)
+                nc.tensor.matmul_mx(
+                    out=s_ps[:],
+                    lhsT=z_codes[:, cols].bitcast(FP8X4),
+                    lhsT_scale=z_sc[:, cols],
+                    rhs=z2_codes[:].bitcast(FP8X4),
+                    rhs_scale=z2_sc[:],
+                    start=True,
+                    stop=True,
+                )
+                nc.vector.tensor_scalar(s_win[t][:, places], s_ps[:], 0.0625, None, ALU.mult)
+            for t in range(PACK):
+                nc.vector.tensor_tensor(s_sq[t][:, places], s_win[t][:, places], s_win[t][:, places], ALU.mult)
+
+        out_rows = out.rearrange("(p t) j -> p t j", t=PACK)
+
+        def fetch(t, lo, hi):
+            pa2 = ring.tile([P, hi - lo], F32, name="pa2")
+            nc.scalar.activation(pa2[:], s_win[t][:].indirect(n6_sb[:, lo // 16 : hi // 16]), ACT.Copy)
+            pa2_sq = ring.tile([P, hi - lo], F32, name="pa2_sq")
+            nc.scalar.activation(pa2_sq[:], pa2[:], ACT.Square)
+            top = ring.tile([P, hi - lo], F32, name="top", bufs=3)
+            nc.vector.scalar_tensor_tensor(top[:], pa2[:], 2.0, s_win[t][:, lo:hi], ALU.mult, ALU.mult)
+            bottom = ring.tile([P, hi - lo], F32, name="bottom", bufs=3)
+            nc.vector.scalar_tensor_tensor(bottom[:], pa2_sq[:], 0.5, s_sq[t][:, lo:hi], ALU.add, ALU.add)
+            return top, bottom
+
+        def divide(t, lo, hi, top, bottom):
+            root = ring.tile([P, hi - lo], F32, name="root")
+            nc.scalar.activation(root[:], bottom[:], ACT.Abs_reciprocal_sqrt)
+            once = ring.tile([P, hi - lo], F32, name="once")
+            result = ring.tile([P, hi - lo], F32, name="result", bufs=5)
+            if t == PACK - 1:
+                nc.scalar.activation(once[:], root[:], ACT.Square)
+                nc.vector.tensor_tensor(result[:], once[:], top[:], ALU.mult)
+            else:
+                nc.vector.tensor_tensor(once[:], top[:], root[:], ALU.mult)
+                nc.vector.tensor_tensor(result[:], once[:], root[:], ALU.mult)
+            nc.sync.dma_start(out_rows[:, t, lo:hi], result[:])
+
+        steps = [(0, 0, S), (1, 0, S), (2, 0, S), (3, 0, W), (3, W, S)]
+        waiting = fetch(*steps[0])
+        for i in range(len(steps)):
+            ahead = fetch(*steps[i + 1]) if i + 1 < len(steps) else None
+            divide(*steps[i], *waiting)
+            waiting = ahead

@@ -19,6 +19,7 @@ ALU = mybir.AluOpType
 P = 128
 PACK = 4
 CHUNK = 256
+LEAD = 2
 
 
 def tile_picked_selffilloddsharm_none_p_kernel(
@@ -38,10 +39,10 @@ def tile_picked_selffilloddsharm_none_p_kernel(
 
         table_scales = keep.tile([P, T], U8, name="table_scales")
         nc.gpsimd.memset(table_scales[:].bitcast(I32), 0)
-        offs_sb = load_list("offs_sb", offs)
         w_rows = w1.rearrange("(p j) c -> p j c", j=PACK)
         w_raw = [keep.tile([P, PACK, H // 2], F32, name="w_raw%d" % h) for h in range(2)]
         nc.sync.dma_start(w_raw[0][:], w_rows[:, :, : H // 2])
+        offs_sb = load_list("offs_sb", offs)
         for q in range(4):
             nc.sync.dma_start(
                 table_scales[32 * q : 32 * q + 4, :].bitcast(I32), x_scales[0, 4 * q : 4 * q + 4, :].bitcast(I32)
@@ -110,15 +111,17 @@ def tile_picked_selffilloddsharm_none_p_kernel(
             nc.vector.tensor_tensor(ra[:], pa[:], pb[:], ALU.max)
             nc.vector.tensor_copy(y[t][:].indirect(n1_sb[:]), ra[:])
             nc.vector.tensor_scalar(z_planes[:, t, :], y[t][:], ga_sb[:, t : t + 1], None, ALU.mult)
-        z_bf = keep.tile([P, PACK, P, PACK], BF16, name="z_bf", align_bytes=64)
         z_codes = keep.tile([P, S], U32, name="z_codes", align_bytes=64)
         z_sc = keep.tile([P, S], U8, name="z_sc", align_bytes=64)
-        nc.vector.tensor_copy(
-            z_bf[:].rearrange("p t m j -> p m j t"), z_planes[:].rearrange("p j (m t) -> p m j t", t=PACK)
-        )
-        nc.vector.quantize_mx(
-            out=z_codes[:].bitcast(FP8X4), scales=z_sc[:], in_=z_bf[:].rearrange("p t m j -> p (t m j)")
-        )
+
+        def quantise_z():
+            z_bf = ring.tile([P, PACK, P, PACK], BF16, name="z_bf", tag="z_bf", bufs=1, align_bytes=64)
+            nc.vector.tensor_copy(
+                z_bf[:].rearrange("p t m j -> p m j t"), z_planes[:].rearrange("p j (m t) -> p m j t", t=PACK)
+            )
+            nc.vector.quantize_mx(
+                out=z_codes[:].bitcast(FP8X4), scales=z_sc[:], in_=z_bf[:].rearrange("p t m j -> p (t m j)")
+            )
 
         s_win = [keep.tile([P, 2 * S], F32, name="s_win%d" % t) for t in range(PACK)]
         for t in range(PACK):
@@ -129,10 +132,48 @@ def tile_picked_selffilloddsharm_none_p_kernel(
         def turn(bank, t, source, start, stop):
             nc.tensor.matmul(bank[:, t, :], lhsT=source, rhs=ident[:], start=start, stop=stop, is_transpose=True)
 
-        for c in range(S // CHUNK):
+        chunks = S // CHUNK
+        codes = []
+
+        def second_product(c):
+            places = slice(c * CHUNK, (c + 1) * CHUNK)
+            z2_codes, z2_sc = codes[c]
+            for t in range(PACK):
+                s_ps = psum.tile([P, CHUNK], F32, name="s_ps", tag="bank%d" % (((2, 3, 2, 3), (2, 3, 5, 6)))[c][t])
+                cols = slice(t * P, (t + 1) * P)
+                nc.tensor.matmul_mx(
+                    out=s_ps[:],
+                    lhsT=z_codes[:, cols].bitcast(FP8X4),
+                    lhsT_scale=z_sc[:, cols],
+                    rhs=z2_codes[:].bitcast(FP8X4),
+                    rhs_scale=z2_sc[:],
+                    start=True,
+                    stop=True,
+                )
+                if False:
+                    nc.scalar.activation(s_win[t][:, places], s_ps[:], ACT.Copy, scale=0.0625)
+                else:
+                    nc.vector.tensor_scalar(s_win[t][:, places], s_ps[:], 0.0625, None, ALU.mult)
+            for t in range(PACK):
+                nc.vector.tensor_tensor(s_sq[t][:, places], s_win[t][:, places], s_win[t][:, places], ALU.mult)
+
+        quantise_z()
+        for c in range(chunks):
+            last = c + 1 == chunks
             entries = slice(c * CHUNK // 16, (c + 1) * CHUNK // 16)
+            sums = [(0, 0, PACK, 6), (1, 0, PACK - 1, 7), (1, PACK - 1, 1, 4)] if last else [(0, 0, PACK, 6), (1, 0, PACK, 7)]
+            num = []
+
+            def open_sum(b, t0, planes, bank):
+                tile = psum.tile([P, planes, P], F32, name="num", tag="bank%d" % bank)
+                first = c * CHUNK + b * P
+                for i in range(planes):
+                    turn(tile, i, ex[t0 + i][:, first : first + P], i == 0, False)
+                num.append(tile)
+
+            for part in sums[:blocks]:
+                open_sum(*part)
             den = [psum.tile([P, PACK, P], F32, name="den", tag="bank%d" % (4 + b)) for b in range(blocks)]
-            num = [psum.tile([P, PACK, P], F32, name="num", tag="bank%d" % (6 + b)) for b in range(blocks)]
             for t in range(PACK):
                 e4 = ring.tile([P, CHUNK], F32, name="e4", bufs=4)
                 nc.scalar.activation(e4[:], ex[t][:].indirect(n4_sb[:, entries]), ACT.Copy)
@@ -142,30 +183,50 @@ def tile_picked_selffilloddsharm_none_p_kernel(
                     turn(den[b], t, e4[:, b * P : (b + 1) * P], True, False)
                 for b in range(blocks):
                     turn(den[b], t, e5[:, b * P : (b + 1) * P], False, True)
+            ln_den = []
             for b in range(blocks):
-                first = c * CHUNK + b * P
-                for t in range(PACK):
-                    turn(num[b], t, ex[t][:, first : first + P], t == 0, False)
-            for t in range(PACK):
-                e3 = ring.tile([P, CHUNK], F32, name="e3", bufs=4)
-                nc.scalar.activation(e3[:], ex[t][:].indirect(n3_sb[:, entries]), ACT.Copy)
-                for b in range(blocks):
-                    turn(num[b], t, e3[:, b * P : (b + 1) * P], False, t == PACK - 1)
+                tile = ring.tile([P, PACK, P], F32, name="ln_den")
+                nc.scalar.activation(tile[:], den[b][:], ACT.Ln)
+                ln_den.append(tile)
             back = [psum.tile([P, PACK, P], F32, name="back", tag="bank%d" % b) for b in range(blocks)]
-            for b in range(blocks):
-                ln_den = ring.tile([P, PACK, P], F32, name="ln_den")
-                nc.scalar.activation(ln_den[:], den[b][:], ACT.Ln)
+            if last:
                 minus = ring.tile([P, PACK, P], F32, name="minus")
-                nc.vector.tensor_scalar(minus[:], ln_den[:], -1.0, None, ALU.mult)
+                nc.vector.tensor_scalar(minus[:], ln_den[1][:], -1.0, None, ALU.mult)
                 for t in range(PACK):
-                    turn(back[b], t, minus[:, t, :], t == 0, False)
+                    turn(back[1], t, minus[:, t, :], t == 0, False)
+            for part in sums[blocks:]:
+                open_sum(*part)
+            ln_num = []
+            for group in [[0], [1]] if last else [[0, 1]]:
+                lo = c * CHUNK + group[0] * P
+                width = len(group) * P
+                for t in range(PACK):
+                    e3 = ring.tile([P, width], F32, name="e3", bufs=4)
+                    nc.scalar.activation(e3[:], ex[t][:].indirect(n3_sb[:, lo // 16 : (lo + width) // 16]), ACT.Copy)
+                    for tile, (b, t0, planes, bank) in zip(num, sums):
+                        if b in group and t0 <= t < t0 + planes:
+                            at = (b - group[0]) * P
+                            turn(tile, t - t0, e3[:, at : at + P], False, t == t0 + planes - 1)
+                for tile, (b, t0, planes, bank) in zip(num, sums):
+                    if b in group:
+                        logs = ring.tile([P, planes, P], F32, name="ln_num", bufs=3)
+                        nc.scalar.activation(logs[:], tile[:], ACT.Ln)
+                        ln_num.append(logs)
+            if last:
+                warm = keep.tile([P, 1], F32, name="warm")
+                nc.scalar.activation(warm[:], num[-1][:, 0, 0:1], ACT.Abs_reciprocal_sqrt)
             z2_codes = ring.tile([P, CHUNK], U32, name="z2_codes", align_bytes=64)
             z2_sc = ring.tile([P, CHUNK], U8, name="z2_sc", align_bytes=64)
             for b in range(blocks):
-                ln_num = ring.tile([P, PACK, P], F32, name="ln_num")
-                nc.scalar.activation(ln_num[:], num[b][:], ACT.Ln)
-                for t in range(PACK):
-                    turn(back[b], t, ln_num[:, t, :], False, t == PACK - 1)
+                if last and b == 1:
+                    for logs, (bb, t0, planes, bank) in zip(ln_num[1:], sums[1:]):
+                        for i in range(planes):
+                            turn(back[1], t0 + i, logs[:, i, :], False, t0 + i == PACK - 1)
+                else:
+                    ln_q = ring.tile([P, PACK, P], F32, name="ln_q")
+                    nc.vector.tensor_tensor(ln_q[:], ln_num[b][:], ln_den[b][:], ALU.subtract)
+                    for t in range(PACK):
+                        turn(back[b], t, ln_q[:, t, :], True, True)
                 z2_bf = ring.tile([P, P, PACK], BF16, name="z2_bf", align_bytes=64)
                 nc.vector.tensor_tensor(
                     z2_bf[:],
@@ -178,33 +239,26 @@ def tile_picked_selffilloddsharm_none_p_kernel(
                     scales=z2_sc[:, b * P : (b + 1) * P],
                     in_=z2_bf[:].rearrange("p j t -> p (j t)"),
                 )
-            places = slice(c * CHUNK, (c + 1) * CHUNK)
-            for t in range(PACK):
-                s_ps = psum.tile([P, CHUNK], F32, name="s_ps", tag="bank%d" % (2 + t % 2))
-                cols = slice(t * P, (t + 1) * P)
-                nc.tensor.matmul_mx(
-                    out=s_ps[:],
-                    lhsT=z_codes[:, cols].bitcast(FP8X4),
-                    lhsT_scale=z_sc[:, cols],
-                    rhs=z2_codes[:].bitcast(FP8X4),
-                    rhs_scale=z2_sc[:],
-                    start=True,
-                    stop=True,
-                )
-                nc.vector.tensor_scalar(s_win[t][:, places], s_ps[:], 0.0625, None, ALU.mult)
-            for t in range(PACK):
-                nc.vector.tensor_tensor(s_sq[t][:, places], s_win[t][:, places], s_win[t][:, places], ALU.mult)
+            if last:
+                second_product(c - 1)
+            codes.append((z2_codes, z2_sc))
+            if False:
+                second_product(c)
+        second_product(chunks - 1)
 
         out_rows = out.rearrange("(p t) j -> p t j", t=PACK)
 
         def fetch(t, lo, hi):
-            pa2 = ring.tile([P, hi - lo], F32, name="pa2")
+            pa2 = ring.tile([P, hi - lo], F32, name="pa2", bufs=2)
             nc.scalar.activation(pa2[:], s_win[t][:].indirect(n6_sb[:, lo // 16 : hi // 16]), ACT.Copy)
-            pa2_sq = ring.tile([P, hi - lo], F32, name="pa2_sq")
-            nc.scalar.activation(pa2_sq[:], pa2[:], ACT.Square)
-            top = ring.tile([P, hi - lo], F32, name="top", bufs=3)
+            pa2_sq = ring.tile([P, hi - lo], F32, name="pa2_sq", bufs=2)
+            if t < 1:
+                nc.vector.tensor_tensor(pa2_sq[:], pa2[:], pa2[:], ALU.mult)
+            else:
+                nc.scalar.activation(pa2_sq[:], pa2[:], ACT.Square)
+            top = ring.tile([P, hi - lo], F32, name="top", bufs=4)
             nc.vector.scalar_tensor_tensor(top[:], pa2[:], 2.0, s_win[t][:, lo:hi], ALU.mult, ALU.mult)
-            bottom = ring.tile([P, hi - lo], F32, name="bottom", bufs=3)
+            bottom = ring.tile([P, hi - lo], F32, name="bottom", bufs=4)
             nc.vector.scalar_tensor_tensor(bottom[:], pa2_sq[:], 0.5, s_sq[t][:, lo:hi], ALU.add, ALU.add)
             return top, bottom
 
@@ -212,8 +266,8 @@ def tile_picked_selffilloddsharm_none_p_kernel(
             root = ring.tile([P, hi - lo], F32, name="root")
             nc.scalar.activation(root[:], bottom[:], ACT.Abs_reciprocal_sqrt)
             once = ring.tile([P, hi - lo], F32, name="once")
-            result = ring.tile([P, hi - lo], F32, name="result", bufs=5)
-            if t == PACK - 1:
+            result = ring.tile([P, hi - lo], F32, name="result", bufs=8)
+            if t >= 2:
                 nc.scalar.activation(once[:], root[:], ACT.Square)
                 nc.vector.tensor_tensor(result[:], once[:], top[:], ALU.mult)
             else:
@@ -222,8 +276,8 @@ def tile_picked_selffilloddsharm_none_p_kernel(
             nc.sync.dma_start(out_rows[:, t, lo:hi], result[:])
 
         steps = [(0, 0, S), (1, 0, S), (2, 0, S), (3, 0, W), (3, W, S)]
-        waiting = fetch(*steps[0])
-        for i in range(len(steps)):
-            ahead = fetch(*steps[i + 1]) if i + 1 < len(steps) else None
-            divide(*steps[i], *waiting)
-            waiting = ahead
+        fetched = [fetch(*step) for step in steps[:LEAD]]
+        for i, step in enumerate(steps):
+            if i + LEAD < len(steps):
+                fetched.append(fetch(*steps[i + LEAD]))
+            divide(*step, *fetched[i])

@@ -17,9 +17,19 @@ ACT = mybir.ActivationFunctionType
 ALU = mybir.AluOpType
 
 P = 128
-PACK = 4
-CHUNK = 256
+PLANES = 4
+PER_COLUMN = 16
+HALF = S // 2
+STRIPS = HALF // P
+
 LEAD = 2
+VECTOR_SQUARES_PA2 = 1
+SCALAR_SQUARES_ROOT = 2
+
+BACK_BANK = 0
+S_BANKS = ((2, 3, 2, 3), (2, 3, 5, 6))
+DEN_BANK = 4
+NUM_BANK = 6
 
 
 def tile_picked_selffilloddsharm_none_p_kernel(
@@ -37,10 +47,28 @@ def tile_picked_selffilloddsharm_none_p_kernel(
             nc.sync.dma_start(tile[:], source)
             return tile
 
+        def entries(tile, lo, hi):
+            return tile[:, lo // PER_COLUMN : hi // PER_COLUMN]
+
+        def bank_tile(shape, name, bank):
+            return psum.tile(shape, F32, name=name, tag="bank%d" % bank)
+
+        def product(result, codes, scales, t, moving_codes, moving_scales):
+            dealt = slice(t * P, (t + 1) * P)
+            nc.tensor.matmul_mx(
+                out=result,
+                lhsT=codes[:, dealt].bitcast(FP8X4),
+                lhsT_scale=scales[:, dealt],
+                rhs=moving_codes.bitcast(FP8X4),
+                rhs_scale=moving_scales,
+                start=True,
+                stop=True,
+            )
+
         table_scales = keep.tile([P, T], U8, name="table_scales")
         nc.gpsimd.memset(table_scales[:].bitcast(I32), 0)
-        w_rows = w1.rearrange("(p j) c -> p j c", j=PACK)
-        w_raw = [keep.tile([P, PACK, H // 2], F32, name="w_raw%d" % h) for h in range(2)]
+        w_rows = w1.rearrange("(p j) c -> p j c", j=PLANES)
+        w_raw = [keep.tile([P, PLANES, H // 2], F32, name="w_raw%d" % h) for h in range(2)]
         nc.sync.dma_start(w_raw[0][:], w_rows[:, :, : H // 2])
         offs_sb = load_list("offs_sb", offs)
         for q in range(4):
@@ -55,19 +83,22 @@ def tile_picked_selffilloddsharm_none_p_kernel(
         n4_sb = load_list("n4_sb", n4)
         n5_sb = load_list("n5_sb", n5)
         n3_sb = load_list("n3_sb", n3)
-        ga_sb = keep.tile([P, PACK], F32, name="ga_sb")
-        nc.sync.dma_start(ga_sb[:], ga.rearrange("(p t) o -> p (t o)", t=PACK))
-        gb_sb = keep.tile([P, PACK], F32, name="gb_sb")
-        nc.sync.dma_start(gb_sb[:], gb.rearrange("(p t) o -> p (t o)", t=PACK))
+        ga_sb = keep.tile([P, PLANES], F32, name="ga_sb")
+        nc.sync.dma_start(ga_sb[:], ga.rearrange("(p t) o -> p (t o)", t=PLANES))
+        gb_sb = keep.tile([P, PLANES], F32, name="gb_sb")
+        nc.sync.dma_start(gb_sb[:], gb.rearrange("(p t) o -> p (t o)", t=PLANES))
         n6_sb = load_list("n6_sb", n6)
         ident = keep.tile([P, P], F32, name="ident")
         make_identity(nc, ident[:])
 
-        w_bf = keep.tile([P, PACK, P, PACK], BF16, name="w_bf", align_bytes=64)
+        def turn(bank, slot, source, start, stop):
+            nc.tensor.matmul(bank[:, slot, :], lhsT=source, rhs=ident[:], start=start, stop=stop, is_transpose=True)
+
+        w_bf = keep.tile([P, PLANES, P, PLANES], BF16, name="w_bf", align_bytes=64)
         for h in range(2):
             nc.scalar.activation(
-                w_bf[:, :, h * 64 : (h + 1) * 64, :].rearrange("p t m j -> p m j t"),
-                w_raw[h][:].rearrange("p j (m t) -> p m j t", t=PACK),
+                w_bf[:, :, h * (P // 2) : (h + 1) * (P // 2), :].rearrange("p t m j -> p m j t"),
+                w_raw[h][:].rearrange("p j (m t) -> p m j t", t=PLANES),
                 ACT.Copy,
             )
         x_sc = keep.tile([P, S], U8, name="x_sc", align_bytes=64)
@@ -77,207 +108,184 @@ def tile_picked_selffilloddsharm_none_p_kernel(
         nc.vector.quantize_mx(
             out=w_codes[:].bitcast(FP8X4), scales=w_sc[:], in_=w_bf[:].rearrange("p t m j -> p (t m j)")
         )
-        x_codes = keep.tile([P, S], U32, name="x_codes", align_bytes=64)
-        for h in range(2):
-            nc.vector.tensor_copy(
-                x_codes[:, h * W : (h + 1) * W], table_words[:].indirect(offs_sb[:, h * 16 : (h + 1) * 16])
-            )
 
-        ex = [keep.tile([P, S], F32, name="ex%d" % t) for t in range(PACK)]
-        y = [keep.tile([P, S], F32, name="y%d" % t) for t in range(PACK)]
-        pieces = [(0, 0, W), (1, 0, W), (0, W, S), (1, W, S), (2, 0, S), (3, 0, S)]
-        for bank, (t, lo, hi) in enumerate(pieces):
-            y_ps = psum.tile([P, hi - lo], F32, name="y_ps", tag="bank%d" % bank)
-            cols = slice(t * P, (t + 1) * P)
-            nc.tensor.matmul_mx(
-                out=y_ps[:],
-                lhsT=w_codes[:, cols].bitcast(FP8X4),
-                lhsT_scale=w_sc[:, cols],
-                rhs=x_codes[:, lo:hi].bitcast(FP8X4),
-                rhs_scale=x_sc[:, lo:hi],
-                start=True,
-                stop=True,
-            )
+        x_codes = keep.tile([P, S], U32, name="x_codes", align_bytes=64)
+        for lo in (0, HALF):
+            nc.vector.tensor_copy(x_codes[:, lo : lo + HALF], table_words[:].indirect(entries(offs_sb, lo, lo + HALF)))
+        ex = [keep.tile([P, S], F32, name="ex%d" % t) for t in range(PLANES)]
+        y = [keep.tile([P, S], F32, name="y%d" % t) for t in range(PLANES)]
+        y_pieces = [(t, lo, lo + HALF) for lo in (0, HALF) for t in (0, 1)] + [(t, 0, S) for t in (2, 3)]
+        for bank, (t, lo, hi) in enumerate(y_pieces):
+            y_ps = bank_tile([P, hi - lo], "y_ps", bank)
+            product(y_ps[:], w_codes, w_sc, t, x_codes[:, lo:hi], x_sc[:, lo:hi])
             nc.scalar.activation(ex[t][:, lo:hi], y_ps[:], ACT.Exp, scale=0.5)
             nc.vector.tensor_copy(y[t][:, lo:hi], y_ps[:])
 
-        z_planes = keep.tile([P, PACK, S], BF16, name="z_planes")
-        for t in range(PACK):
-            pb = ring.tile([P, W], F32, name="pb", bufs=4)
+        z_planes = keep.tile([P, PLANES, S], BF16, name="z_planes")
+        for t in range(PLANES):
+            pb = ring.tile([P, W], F32, name="pb", bufs=PLANES)
             nc.scalar.activation(pb[:], y[t][:].indirect(n2_sb[:]), ACT.Copy)
-            pa = ring.tile([P, W], F32, name="pa", bufs=4)
+            pa = ring.tile([P, W], F32, name="pa", bufs=PLANES)
             nc.vector.tensor_copy(pa[:], y[t][:].indirect(n1_sb[:]))
             ra = ring.tile([P, W], F32, name="ra")
             nc.vector.tensor_tensor(ra[:], pa[:], pb[:], ALU.max)
             nc.vector.tensor_copy(y[t][:].indirect(n1_sb[:]), ra[:])
             nc.vector.tensor_scalar(z_planes[:, t, :], y[t][:], ga_sb[:, t : t + 1], None, ALU.mult)
+
+        s_win = [keep.tile([P, 2 * S], F32, name="s_win%d" % t) for t in range(PLANES)]
+        for t in range(PLANES):
+            nc.gpsimd.memset(s_win[t][:, S:], 0.0)
+        s_sq = [keep.tile([P, S], F32, name="s_sq%d" % t) for t in range(PLANES)]
+
+        z_bf = keep.tile([P, PLANES, P, PLANES], BF16, name="z_bf", align_bytes=64)
+        nc.vector.tensor_copy(
+            z_bf[:].rearrange("p t m j -> p m j t"), z_planes[:].rearrange("p j (m t) -> p m j t", t=PLANES)
+        )
         z_codes = keep.tile([P, S], U32, name="z_codes", align_bytes=64)
         z_sc = keep.tile([P, S], U8, name="z_sc", align_bytes=64)
+        nc.vector.quantize_mx(
+            out=z_codes[:].bitcast(FP8X4), scales=z_sc[:], in_=z_bf[:].rearrange("p t m j -> p (t m j)")
+        )
 
-        def quantise_z():
-            z_bf = ring.tile([P, PACK, P, PACK], BF16, name="z_bf", tag="z_bf", bufs=1, align_bytes=64)
-            nc.vector.tensor_copy(
-                z_bf[:].rearrange("p t m j -> p m j t"), z_planes[:].rearrange("p j (m t) -> p m j t", t=PACK)
+        def open_numerators(strip, planes, bank):
+            num = bank_tile([P, len(planes), P], "num", bank)
+            for slot, t in enumerate(planes):
+                turn(num, slot, ex[t][:, strip * P : (strip + 1) * P], slot == 0, False)
+            return strip, planes, num
+
+        def close_numerators(lo, hi, opened):
+            for t in range(PLANES):
+                e3 = ring.tile([P, hi - lo], F32, name="e3", bufs=PLANES)
+                nc.scalar.activation(e3[:], ex[t][:].indirect(entries(n3_sb, lo, hi)), ACT.Copy)
+                for strip, planes, num in opened:
+                    if t in planes:
+                        at = strip * P - lo
+                        turn(num, planes.index(t), e3[:, at : at + P], False, t == planes[-1])
+            ln_nums = []
+            for strip, planes, num in opened:
+                ln_num = ring.tile([P, len(planes), P], F32, name="ln_num", bufs=3)
+                nc.scalar.activation(ln_num[:], num[:], ACT.Ln)
+                ln_nums.append(ln_num)
+            return ln_nums
+
+        def denominators(half):
+            lo, hi = half * HALF, (half + 1) * HALF
+            den = [bank_tile([P, PLANES, P], "den", DEN_BANK + b) for b in range(STRIPS)]
+            for t in range(PLANES):
+                e4 = ring.tile([P, HALF], F32, name="e4", bufs=PLANES)
+                nc.scalar.activation(e4[:], ex[t][:].indirect(entries(n4_sb, lo, hi)), ACT.Copy)
+                e5 = ring.tile([P, HALF], F32, name="e5", bufs=PLANES)
+                nc.scalar.activation(e5[:], ex[t][:].indirect(entries(n5_sb, lo, hi)), ACT.Copy)
+                for b in range(STRIPS):
+                    turn(den[b], t, e4[:, b * P : (b + 1) * P], True, False)
+                for b in range(STRIPS):
+                    turn(den[b], t, e5[:, b * P : (b + 1) * P], False, True)
+            ln_dens = []
+            for b in range(STRIPS):
+                ln_den = ring.tile([P, PLANES, P], F32, name="ln_den")
+                nc.scalar.activation(ln_den[:], den[b][:], ACT.Ln)
+                ln_dens.append(ln_den)
+            return ln_dens
+
+        def subtract_and_turn_back(ln_num, ln_den, back):
+            ln_q = ring.tile([P, PLANES, P], F32, name="ln_q")
+            nc.vector.tensor_tensor(ln_q[:], ln_num[:], ln_den[:], ALU.subtract)
+            for t in range(PLANES):
+                turn(back, t, ln_q[:, t, :], True, True)
+
+        def quantise_strip(back, z2_codes, z2_sc, b):
+            z2_bf = ring.tile([P, P, PLANES], BF16, name="z2_bf", align_bytes=64)
+            nc.vector.tensor_tensor(
+                z2_bf[:],
+                back[:].rearrange("p t j -> p j t"),
+                gb_sb[:].unsqueeze(1).to_broadcast([P, P, PLANES]),
+                ALU.mult,
             )
             nc.vector.quantize_mx(
-                out=z_codes[:].bitcast(FP8X4), scales=z_sc[:], in_=z_bf[:].rearrange("p t m j -> p (t m j)")
+                out=z2_codes[:, b * P : (b + 1) * P].bitcast(FP8X4),
+                scales=z2_sc[:, b * P : (b + 1) * P],
+                in_=z2_bf[:].rearrange("p j t -> p (j t)"),
             )
 
-        s_win = [keep.tile([P, 2 * S], F32, name="s_win%d" % t) for t in range(PACK)]
-        for t in range(PACK):
-            nc.gpsimd.memset(s_win[t][:, S:], 0.0)
-        s_sq = [keep.tile([P, S], F32, name="s_sq%d" % t) for t in range(PACK)]
-        blocks = CHUNK // P
-
-        def turn(bank, t, source, start, stop):
-            nc.tensor.matmul(bank[:, t, :], lhsT=source, rhs=ident[:], start=start, stop=stop, is_transpose=True)
-
-        chunks = S // CHUNK
-        codes = []
-
-        def second_product(c):
-            places = slice(c * CHUNK, (c + 1) * CHUNK)
-            z2_codes, z2_sc = codes[c]
-            for t in range(PACK):
-                s_ps = psum.tile([P, CHUNK], F32, name="s_ps", tag="bank%d" % (((2, 3, 2, 3), (2, 3, 5, 6)))[c][t])
-                cols = slice(t * P, (t + 1) * P)
-                nc.tensor.matmul_mx(
-                    out=s_ps[:],
-                    lhsT=z_codes[:, cols].bitcast(FP8X4),
-                    lhsT_scale=z_sc[:, cols],
-                    rhs=z2_codes[:].bitcast(FP8X4),
-                    rhs_scale=z2_sc[:],
-                    start=True,
-                    stop=True,
-                )
-                if False:
-                    nc.scalar.activation(s_win[t][:, places], s_ps[:], ACT.Copy, scale=0.0625)
-                else:
-                    nc.vector.tensor_scalar(s_win[t][:, places], s_ps[:], 0.0625, None, ALU.mult)
-            for t in range(PACK):
+        def second_product(half, z2_codes, z2_sc):
+            places = slice(half * HALF, (half + 1) * HALF)
+            for t in range(PLANES):
+                s_ps = bank_tile([P, HALF], "s_ps", S_BANKS[half][t])
+                product(s_ps[:], z_codes, z_sc, t, z2_codes[:], z2_sc[:])
+                nc.vector.tensor_scalar(s_win[t][:, places], s_ps[:], 0.0625, None, ALU.mult)
+            for t in range(PLANES):
                 nc.vector.tensor_tensor(s_sq[t][:, places], s_win[t][:, places], s_win[t][:, places], ALU.mult)
 
-        quantise_z()
-        for c in range(chunks):
-            last = c + 1 == chunks
-            entries = slice(c * CHUNK // 16, (c + 1) * CHUNK // 16)
-            sums = [(0, 0, PACK, 6), (1, 0, PACK - 1, 7), (1, PACK - 1, 1, 4)] if last else [(0, 0, PACK, 6), (1, 0, PACK, 7)]
-            num = []
+        all_planes = list(range(PLANES))
+        z2_codes = [keep.tile([P, HALF], U32, name="z2_codes%d" % half, align_bytes=64) for half in range(2)]
+        z2_sc = [keep.tile([P, HALF], U8, name="z2_sc%d" % half, align_bytes=64) for half in range(2)]
 
-            def open_sum(b, t0, planes, bank):
-                tile = psum.tile([P, planes, P], F32, name="num", tag="bank%d" % bank)
-                first = c * CHUNK + b * P
-                for i in range(planes):
-                    turn(tile, i, ex[t0 + i][:, first : first + P], i == 0, False)
-                num.append(tile)
+        opened = [open_numerators(b, all_planes, NUM_BANK + b) for b in range(STRIPS)]
+        ln_dens = denominators(0)
+        ln_nums = close_numerators(0, HALF, opened)
+        for b in range(STRIPS):
+            back = bank_tile([P, PLANES, P], "back", BACK_BANK + b)
+            subtract_and_turn_back(ln_nums[b], ln_dens[b], back)
+            quantise_strip(back, z2_codes[0], z2_sc[0], b)
 
-            for part in sums[:blocks]:
-                open_sum(*part)
-            den = [psum.tile([P, PACK, P], F32, name="den", tag="bank%d" % (4 + b)) for b in range(blocks)]
-            for t in range(PACK):
-                e4 = ring.tile([P, CHUNK], F32, name="e4", bufs=4)
-                nc.scalar.activation(e4[:], ex[t][:].indirect(n4_sb[:, entries]), ACT.Copy)
-                e5 = ring.tile([P, CHUNK], F32, name="e5", bufs=4)
-                nc.scalar.activation(e5[:], ex[t][:].indirect(n5_sb[:, entries]), ACT.Copy)
-                for b in range(blocks):
-                    turn(den[b], t, e4[:, b * P : (b + 1) * P], True, False)
-                for b in range(blocks):
-                    turn(den[b], t, e5[:, b * P : (b + 1) * P], False, True)
-            ln_den = []
-            for b in range(blocks):
-                tile = ring.tile([P, PACK, P], F32, name="ln_den")
-                nc.scalar.activation(tile[:], den[b][:], ACT.Ln)
-                ln_den.append(tile)
-            back = [psum.tile([P, PACK, P], F32, name="back", tag="bank%d" % b) for b in range(blocks)]
-            if last:
-                minus = ring.tile([P, PACK, P], F32, name="minus")
-                nc.vector.tensor_scalar(minus[:], ln_den[1][:], -1.0, None, ALU.mult)
-                for t in range(PACK):
-                    turn(back[1], t, minus[:, t, :], t == 0, False)
-            for part in sums[blocks:]:
-                open_sum(*part)
-            ln_num = []
-            for group in [[0], [1]] if last else [[0, 1]]:
-                lo = c * CHUNK + group[0] * P
-                width = len(group) * P
-                for t in range(PACK):
-                    e3 = ring.tile([P, width], F32, name="e3", bufs=4)
-                    nc.scalar.activation(e3[:], ex[t][:].indirect(n3_sb[:, lo // 16 : (lo + width) // 16]), ACT.Copy)
-                    for tile, (b, t0, planes, bank) in zip(num, sums):
-                        if b in group and t0 <= t < t0 + planes:
-                            at = (b - group[0]) * P
-                            turn(tile, t - t0, e3[:, at : at + P], False, t == t0 + planes - 1)
-                for tile, (b, t0, planes, bank) in zip(num, sums):
-                    if b in group:
-                        logs = ring.tile([P, planes, P], F32, name="ln_num", bufs=3)
-                        nc.scalar.activation(logs[:], tile[:], ACT.Ln)
-                        ln_num.append(logs)
-            if last:
-                warm = keep.tile([P, 1], F32, name="warm")
-                nc.scalar.activation(warm[:], num[-1][:, 0, 0:1], ACT.Abs_reciprocal_sqrt)
-            z2_codes = ring.tile([P, CHUNK], U32, name="z2_codes", align_bytes=64)
-            z2_sc = ring.tile([P, CHUNK], U8, name="z2_sc", align_bytes=64)
-            for b in range(blocks):
-                if last and b == 1:
-                    for logs, (bb, t0, planes, bank) in zip(ln_num[1:], sums[1:]):
-                        for i in range(planes):
-                            turn(back[1], t0 + i, logs[:, i, :], False, t0 + i == PACK - 1)
-                else:
-                    ln_q = ring.tile([P, PACK, P], F32, name="ln_q")
-                    nc.vector.tensor_tensor(ln_q[:], ln_num[b][:], ln_den[b][:], ALU.subtract)
-                    for t in range(PACK):
-                        turn(back[b], t, ln_q[:, t, :], True, True)
-                z2_bf = ring.tile([P, P, PACK], BF16, name="z2_bf", align_bytes=64)
-                nc.vector.tensor_tensor(
-                    z2_bf[:],
-                    back[b][:].rearrange("p t j -> p j t"),
-                    gb_sb[:].unsqueeze(1).to_broadcast([P, P, PACK]),
-                    ALU.mult,
-                )
-                nc.vector.quantize_mx(
-                    out=z2_codes[:, b * P : (b + 1) * P].bitcast(FP8X4),
-                    scales=z2_sc[:, b * P : (b + 1) * P],
-                    in_=z2_bf[:].rearrange("p j t -> p (j t)"),
-                )
-            if last:
-                second_product(c - 1)
-            codes.append((z2_codes, z2_sc))
-            if False:
-                second_product(c)
-        second_product(chunks - 1)
+        opened_2 = open_numerators(2, all_planes, NUM_BANK)
+        opened_3 = [open_numerators(3, all_planes[:-1], NUM_BANK + 1)]
+        ln_dens = denominators(1)
+        back_3 = bank_tile([P, PLANES, P], "back", BACK_BANK + 1)
+        minus_ln_den = keep.tile([P, PLANES, P], F32, name="minus_ln_den")
+        nc.vector.tensor_scalar(minus_ln_den[:], ln_dens[1][:], -1.0, None, ALU.mult)
+        for t in range(PLANES):
+            turn(back_3, t, minus_ln_den[:, t, :], t == 0, False)
+        opened_3.append(open_numerators(3, all_planes[-1:], DEN_BANK))
+        (ln_num_2,) = close_numerators(2 * P, 3 * P, [opened_2])
+        ln_nums_3 = close_numerators(3 * P, 4 * P, opened_3)
 
-        out_rows = out.rearrange("(p t) j -> p t j", t=PACK)
+        warm_up = keep.tile([P, 1], F32, name="warm_up")
+        nc.scalar.activation(warm_up[:], opened_3[-1][2][:, 0, 0:1], ACT.Abs_reciprocal_sqrt)
+
+        back_2 = bank_tile([P, PLANES, P], "back", BACK_BANK)
+        subtract_and_turn_back(ln_num_2, ln_dens[0], back_2)
+        quantise_strip(back_2, z2_codes[1], z2_sc[1], 0)
+        for ln_num, (strip, planes, num) in zip(ln_nums_3, opened_3):
+            for slot, t in enumerate(planes):
+                turn(back_3, t, ln_num[:, slot, :], False, t == PLANES - 1)
+        quantise_strip(back_3, z2_codes[1], z2_sc[1], 1)
+
+        for half in range(2):
+            second_product(half, z2_codes[half], z2_sc[half])
+
+        out_rows = out.rearrange("(p t) j -> p t j", t=PLANES)
 
         def fetch(t, lo, hi):
-            pa2 = ring.tile([P, hi - lo], F32, name="pa2", bufs=2)
-            nc.scalar.activation(pa2[:], s_win[t][:].indirect(n6_sb[:, lo // 16 : hi // 16]), ACT.Copy)
-            pa2_sq = ring.tile([P, hi - lo], F32, name="pa2_sq", bufs=2)
-            if t < 1:
+            pa2 = ring.tile([P, hi - lo], F32, name="pa2", bufs=LEAD + 1)
+            nc.scalar.activation(pa2[:], s_win[t][:].indirect(entries(n6_sb, lo, hi)), ACT.Copy)
+            pa2_sq = ring.tile([P, hi - lo], F32, name="pa2_sq")
+            if t < VECTOR_SQUARES_PA2:
                 nc.vector.tensor_tensor(pa2_sq[:], pa2[:], pa2[:], ALU.mult)
             else:
                 nc.scalar.activation(pa2_sq[:], pa2[:], ACT.Square)
-            top = ring.tile([P, hi - lo], F32, name="top", bufs=4)
+            top = ring.tile([P, hi - lo], F32, name="top", bufs=LEAD + 2)
             nc.vector.scalar_tensor_tensor(top[:], pa2[:], 2.0, s_win[t][:, lo:hi], ALU.mult, ALU.mult)
-            bottom = ring.tile([P, hi - lo], F32, name="bottom", bufs=4)
+            bottom = ring.tile([P, hi - lo], F32, name="bottom", bufs=LEAD + 2)
             nc.vector.scalar_tensor_tensor(bottom[:], pa2_sq[:], 0.5, s_sq[t][:, lo:hi], ALU.add, ALU.add)
             return top, bottom
 
         def divide(t, lo, hi, top, bottom):
             root = ring.tile([P, hi - lo], F32, name="root")
             nc.scalar.activation(root[:], bottom[:], ACT.Abs_reciprocal_sqrt)
-            once = ring.tile([P, hi - lo], F32, name="once")
-            result = ring.tile([P, hi - lo], F32, name="result", bufs=8)
-            if t >= 2:
-                nc.scalar.activation(once[:], root[:], ACT.Square)
-                nc.vector.tensor_tensor(result[:], once[:], top[:], ALU.mult)
+            factor = ring.tile([P, hi - lo], F32, name="factor")
+            result = keep.tile([P, hi - lo], F32, name="result%d_%d" % (t, lo))
+            if t >= SCALAR_SQUARES_ROOT:
+                nc.scalar.activation(factor[:], root[:], ACT.Square)
+                nc.vector.tensor_tensor(result[:], factor[:], top[:], ALU.mult)
             else:
-                nc.vector.tensor_tensor(once[:], top[:], root[:], ALU.mult)
-                nc.vector.tensor_tensor(result[:], once[:], root[:], ALU.mult)
+                nc.vector.tensor_tensor(factor[:], top[:], root[:], ALU.mult)
+                nc.vector.tensor_tensor(result[:], factor[:], root[:], ALU.mult)
             nc.sync.dma_start(out_rows[:, t, lo:hi], result[:])
 
-        steps = [(0, 0, S), (1, 0, S), (2, 0, S), (3, 0, W), (3, W, S)]
-        fetched = [fetch(*step) for step in steps[:LEAD]]
-        for i, step in enumerate(steps):
-            if i + LEAD < len(steps):
-                fetched.append(fetch(*steps[i + LEAD]))
-            divide(*step, *fetched[i])
+        out_pieces = [(t, 0, S) for t in range(PLANES - 1)] + [(PLANES - 1, lo, lo + HALF) for lo in (0, HALF)]
+        fetched = [fetch(*piece) for piece in out_pieces[:LEAD]]
+        for i, piece in enumerate(out_pieces):
+            if i + LEAD < len(out_pieces):
+                fetched.append(fetch(*out_pieces[i + LEAD]))
+            divide(*piece, *fetched[i])

from contextlib import ExitStack

import concourse.mybir as mybir
from concourse.masks import make_identity

K, T, S, H, W = 512, 2048, 512, 512, 256
FLOPS = 2 * K * H * S + 2 * H * S * S

F32 = mybir.dt.float32
BF16 = mybir.dt.bfloat16
I32 = mybir.dt.int32
U32 = mybir.dt.uint32
U16 = mybir.dt.uint16
U8 = mybir.dt.uint8
FP8X4 = mybir.dt.float8_e4m3fn_x4
ACT = mybir.ActivationFunctionType
ALU = mybir.AluOpType

P = 128
PLANES = 4
PER_COLUMN = 16
HALF = S // 2
STRIPS = HALF // P

LEAD = 2
VECTOR_SQUARES_PA2 = 1
SCALAR_SQUARES_ROOT = 2

BACK_BANK = 0
S_BANKS = ((2, 3, 2, 3), (2, 3, 5, 6))
DEN_BANK = 4
NUM_BANK = 6


def tile_picked_selffilloddsharm_none_p_kernel(
    tc, x_words, x_scales, w1, ga, gb, offs, n1, n2, n3, n4, n5, n6, out
):
    nc = tc.nc
    with ExitStack() as ctx:
        lists = ctx.enter_context(tc.tile_pool(name="lists", bufs=1))
        keep = ctx.enter_context(tc.tile_pool(name="keep", bufs=1))
        ring = ctx.enter_context(tc.tile_pool(name="ring", bufs=2))
        psum = ctx.enter_context(tc.psum_pool(name="psum", bufs=1))

        def load_list(name, source):
            tile = lists.tile([P, source.shape[1]], U16, name=name)
            nc.sync.dma_start(tile[:], source)
            return tile

        def entries(tile, lo, hi):
            return tile[:, lo // PER_COLUMN : hi // PER_COLUMN]

        def bank_tile(shape, name, bank):
            return psum.tile(shape, F32, name=name, tag="bank%d" % bank)

        def product(result, codes, scales, t, moving_codes, moving_scales):
            dealt = slice(t * P, (t + 1) * P)
            nc.tensor.matmul_mx(
                out=result,
                lhsT=codes[:, dealt].bitcast(FP8X4),
                lhsT_scale=scales[:, dealt],
                rhs=moving_codes.bitcast(FP8X4),
                rhs_scale=moving_scales,
                start=True,
                stop=True,
            )

        table_scales = keep.tile([P, T], U8, name="table_scales")
        nc.gpsimd.memset(table_scales[:].bitcast(I32), 0)
        w_rows = w1.rearrange("(p j) c -> p j c", j=PLANES)
        w_raw = [keep.tile([P, PLANES, H // 2], F32, name="w_raw%d" % h) for h in range(2)]
        nc.sync.dma_start(w_raw[0][:], w_rows[:, :, : H // 2])
        offs_sb = load_list("offs_sb", offs)
        for q in range(4):
            nc.sync.dma_start(
                table_scales[32 * q : 32 * q + 4, :].bitcast(I32), x_scales[0, 4 * q : 4 * q + 4, :].bitcast(I32)
            )
        nc.sync.dma_start(w_raw[1][:], w_rows[:, :, H // 2 :])
        table_words = keep.tile([P, T], U32, name="table_words")
        nc.sync.dma_start(table_words[:].bitcast(I32), x_words[0].rearrange("p n t -> p (n t)").bitcast(I32))
        n2_sb = load_list("n2_sb", n2)
        n1_sb = load_list("n1_sb", n1)
        n4_sb = load_list("n4_sb", n4)
        n5_sb = load_list("n5_sb", n5)
        n3_sb = load_list("n3_sb", n3)
        ga_sb = keep.tile([P, PLANES], F32, name="ga_sb")
        nc.sync.dma_start(ga_sb[:], ga.rearrange("(p t) o -> p (t o)", t=PLANES))
        gb_sb = keep.tile([P, PLANES], F32, name="gb_sb")
        nc.sync.dma_start(gb_sb[:], gb.rearrange("(p t) o -> p (t o)", t=PLANES))
        n6_sb = load_list("n6_sb", n6)
        ident = keep.tile([P, P], F32, name="ident")
        make_identity(nc, ident[:])

        def turn(bank, slot, source, start, stop):
            nc.tensor.matmul(bank[:, slot, :], lhsT=source, rhs=ident[:], start=start, stop=stop, is_transpose=True)

        w_bf = keep.tile([P, PLANES, P, PLANES], BF16, name="w_bf", align_bytes=64)
        for h in range(2):
            nc.scalar.activation(
                w_bf[:, :, h * (P // 2) : (h + 1) * (P // 2), :].rearrange("p t m j -> p m j t"),
                w_raw[h][:].rearrange("p j (m t) -> p m j t", t=PLANES),
                ACT.Copy,
            )
        x_sc = keep.tile([P, S], U8, name="x_sc", align_bytes=64)
        nc.vector.tensor_copy(x_sc[:], table_scales[:].indirect(offs_sb[:]))
        w_codes = keep.tile([P, H], U32, name="w_codes", align_bytes=64)
        w_sc = keep.tile([P, H], U8, name="w_sc", align_bytes=64)
        nc.vector.quantize_mx(
            out=w_codes[:].bitcast(FP8X4), scales=w_sc[:], in_=w_bf[:].rearrange("p t m j -> p (t m j)")
        )

        x_codes = keep.tile([P, S], U32, name="x_codes", align_bytes=64)
        for lo in (0, HALF):
            nc.vector.tensor_copy(x_codes[:, lo : lo + HALF], table_words[:].indirect(entries(offs_sb, lo, lo + HALF)))
        ex = [keep.tile([P, S], F32, name="ex%d" % t) for t in range(PLANES)]
        y = [keep.tile([P, S], F32, name="y%d" % t) for t in range(PLANES)]
        y_pieces = [(t, lo, lo + HALF) for lo in (0, HALF) for t in (0, 1)] + [(t, 0, S) for t in (2, 3)]
        for bank, (t, lo, hi) in enumerate(y_pieces):
            y_ps = bank_tile([P, hi - lo], "y_ps", bank)
            product(y_ps[:], w_codes, w_sc, t, x_codes[:, lo:hi], x_sc[:, lo:hi])
            nc.scalar.activation(ex[t][:, lo:hi], y_ps[:], ACT.Exp, scale=0.5)
            nc.vector.tensor_copy(y[t][:, lo:hi], y_ps[:])

        z_planes = keep.tile([P, PLANES, S], BF16, name="z_planes")
        for t in range(PLANES):
            pb = ring.tile([P, W], F32, name="pb", bufs=PLANES)
            nc.scalar.activation(pb[:], y[t][:].indirect(n2_sb[:]), ACT.Copy)
            pa = ring.tile([P, W], F32, name="pa", bufs=PLANES)
            nc.vector.tensor_copy(pa[:], y[t][:].indirect(n1_sb[:]))
            ra = ring.tile([P, W], F32, name="ra")
            nc.vector.tensor_tensor(ra[:], pa[:], pb[:], ALU.max)
            nc.vector.tensor_copy(y[t][:].indirect(n1_sb[:]), ra[:])
            nc.vector.tensor_scalar(z_planes[:, t, :], y[t][:], ga_sb[:, t : t + 1], None, ALU.mult)

        s_win = [keep.tile([P, 2 * S], F32, name="s_win%d" % t) for t in range(PLANES)]
        for t in range(PLANES):
            nc.gpsimd.memset(s_win[t][:, S:], 0.0)
        s_sq = [keep.tile([P, S], F32, name="s_sq%d" % t) for t in range(PLANES)]

        z_bf = keep.tile([P, PLANES, P, PLANES], BF16, name="z_bf", align_bytes=64)
        nc.vector.tensor_copy(
            z_bf[:].rearrange("p t m j -> p m j t"), z_planes[:].rearrange("p j (m t) -> p m j t", t=PLANES)
        )
        z_codes = keep.tile([P, S], U32, name="z_codes", align_bytes=64)
        z_sc = keep.tile([P, S], U8, name="z_sc", align_bytes=64)
        nc.vector.quantize_mx(
            out=z_codes[:].bitcast(FP8X4), scales=z_sc[:], in_=z_bf[:].rearrange("p t m j -> p (t m j)")
        )

        def open_numerators(strip, planes, bank):
            num = bank_tile([P, len(planes), P], "num", bank)
            for slot, t in enumerate(planes):
                turn(num, slot, ex[t][:, strip * P : (strip + 1) * P], slot == 0, False)
            return strip, planes, num

        def close_numerators(lo, hi, opened):
            for t in range(PLANES):
                e3 = ring.tile([P, hi - lo], F32, name="e3", bufs=PLANES)
                nc.scalar.activation(e3[:], ex[t][:].indirect(entries(n3_sb, lo, hi)), ACT.Copy)
                for strip, planes, num in opened:
                    if t in planes:
                        at = strip * P - lo
                        turn(num, planes.index(t), e3[:, at : at + P], False, t == planes[-1])
            ln_nums = []
            for strip, planes, num in opened:
                ln_num = ring.tile([P, len(planes), P], F32, name="ln_num", bufs=3)
                nc.scalar.activation(ln_num[:], num[:], ACT.Ln)
                ln_nums.append(ln_num)
            return ln_nums

        def denominators(half):
            lo, hi = half * HALF, (half + 1) * HALF
            den = [bank_tile([P, PLANES, P], "den", DEN_BANK + b) for b in range(STRIPS)]
            for t in range(PLANES):
                e4 = ring.tile([P, HALF], F32, name="e4", bufs=PLANES)
                nc.scalar.activation(e4[:], ex[t][:].indirect(entries(n4_sb, lo, hi)), ACT.Copy)
                e5 = ring.tile([P, HALF], F32, name="e5", bufs=PLANES)
                nc.scalar.activation(e5[:], ex[t][:].indirect(entries(n5_sb, lo, hi)), ACT.Copy)
                for b in range(STRIPS):
                    turn(den[b], t, e4[:, b * P : (b + 1) * P], True, False)
                for b in range(STRIPS):
                    turn(den[b], t, e5[:, b * P : (b + 1) * P], False, True)
            ln_dens = []
            for b in range(STRIPS):
                ln_den = ring.tile([P, PLANES, P], F32, name="ln_den")
                nc.scalar.activation(ln_den[:], den[b][:], ACT.Ln)
                ln_dens.append(ln_den)
            return ln_dens

        def subtract_and_turn_back(ln_num, ln_den, back):
            ln_q = ring.tile([P, PLANES, P], F32, name="ln_q")
            nc.vector.tensor_tensor(ln_q[:], ln_num[:], ln_den[:], ALU.subtract)
            for t in range(PLANES):
                turn(back, t, ln_q[:, t, :], True, True)

        def quantise_strip(back, z2_codes, z2_sc, b):
            z2_bf = ring.tile([P, P, PLANES], BF16, name="z2_bf", align_bytes=64)
            nc.vector.tensor_tensor(
                z2_bf[:],
                back[:].rearrange("p t j -> p j t"),
                gb_sb[:].unsqueeze(1).to_broadcast([P, P, PLANES]),
                ALU.mult,
            )
            nc.vector.quantize_mx(
                out=z2_codes[:, b * P : (b + 1) * P].bitcast(FP8X4),
                scales=z2_sc[:, b * P : (b + 1) * P],
                in_=z2_bf[:].rearrange("p j t -> p (j t)"),
            )

        def second_product(half, z2_codes, z2_sc):
            places = slice(half * HALF, (half + 1) * HALF)
            for t in range(PLANES):
                s_ps = bank_tile([P, HALF], "s_ps", S_BANKS[half][t])
                product(s_ps[:], z_codes, z_sc, t, z2_codes[:], z2_sc[:])
                nc.vector.tensor_scalar(s_win[t][:, places], s_ps[:], 0.0625, None, ALU.mult)
            for t in range(PLANES):
                nc.vector.tensor_tensor(s_sq[t][:, places], s_win[t][:, places], s_win[t][:, places], ALU.mult)

        all_planes = list(range(PLANES))
        z2_codes = [keep.tile([P, HALF], U32, name="z2_codes%d" % half, align_bytes=64) for half in range(2)]
        z2_sc = [keep.tile([P, HALF], U8, name="z2_sc%d" % half, align_bytes=64) for half in range(2)]

        opened = [open_numerators(b, all_planes, NUM_BANK + b) for b in range(STRIPS)]
        ln_dens = denominators(0)
        ln_nums = close_numerators(0, HALF, opened)
        for b in range(STRIPS):
            back = bank_tile([P, PLANES, P], "back", BACK_BANK + b)
            subtract_and_turn_back(ln_nums[b], ln_dens[b], back)
            quantise_strip(back, z2_codes[0], z2_sc[0], b)

        opened_2 = open_numerators(2, all_planes, NUM_BANK)
        opened_3 = [open_numerators(3, all_planes[:-1], NUM_BANK + 1)]
        ln_dens = denominators(1)
        back_3 = bank_tile([P, PLANES, P], "back", BACK_BANK + 1)
        minus_ln_den = keep.tile([P, PLANES, P], F32, name="minus_ln_den")
        nc.vector.tensor_scalar(minus_ln_den[:], ln_dens[1][:], -1.0, None, ALU.mult)
        for t in range(PLANES):
            turn(back_3, t, minus_ln_den[:, t, :], t == 0, False)
        opened_3.append(open_numerators(3, all_planes[-1:], DEN_BANK))
        (ln_num_2,) = close_numerators(2 * P, 3 * P, [opened_2])
        ln_nums_3 = close_numerators(3 * P, 4 * P, opened_3)

        warm_up = keep.tile([P, 1], F32, name="warm_up")
        nc.scalar.activation(warm_up[:], opened_3[-1][2][:, 0, 0:1], ACT.Abs_reciprocal_sqrt)

        back_2 = bank_tile([P, PLANES, P], "back", BACK_BANK)
        subtract_and_turn_back(ln_num_2, ln_dens[0], back_2)
        quantise_strip(back_2, z2_codes[1], z2_sc[1], 0)
        for ln_num, (strip, planes, num) in zip(ln_nums_3, opened_3):
            for slot, t in enumerate(planes):
                turn(back_3, t, ln_num[:, slot, :], False, t == PLANES - 1)
        quantise_strip(back_3, z2_codes[1], z2_sc[1], 1)

        for half in range(2):
            second_product(half, z2_codes[half], z2_sc[half])

        out_rows = out.rearrange("(p t) j -> p t j", t=PLANES)

        def fetch(t, lo, hi):
            pa2 = ring.tile([P, hi - lo], F32, name="pa2", bufs=LEAD + 1)
            nc.scalar.activation(pa2[:], s_win[t][:].indirect(entries(n6_sb, lo, hi)), ACT.Copy)
            pa2_sq = ring.tile([P, hi - lo], F32, name="pa2_sq")
            if t < VECTOR_SQUARES_PA2:
                nc.vector.tensor_tensor(pa2_sq[:], pa2[:], pa2[:], ALU.mult)
            else:
                nc.scalar.activation(pa2_sq[:], pa2[:], ACT.Square)
            top = ring.tile([P, hi - lo], F32, name="top", bufs=LEAD + 2)
            nc.vector.scalar_tensor_tensor(top[:], pa2[:], 2.0, s_win[t][:, lo:hi], ALU.mult, ALU.mult)
            bottom = ring.tile([P, hi - lo], F32, name="bottom", bufs=LEAD + 2)
            nc.vector.scalar_tensor_tensor(bottom[:], pa2_sq[:], 0.5, s_sq[t][:, lo:hi], ALU.add, ALU.add)
            return top, bottom

        def divide(t, lo, hi, top, bottom):
            root = ring.tile([P, hi - lo], F32, name="root")
            nc.scalar.activation(root[:], bottom[:], ACT.Abs_reciprocal_sqrt)
            factor = ring.tile([P, hi - lo], F32, name="factor")
            result = keep.tile([P, hi - lo], F32, name="result%d_%d" % (t, lo))
            if t >= SCALAR_SQUARES_ROOT:
                nc.scalar.activation(factor[:], root[:], ACT.Square)
                nc.vector.tensor_tensor(result[:], factor[:], top[:], ALU.mult)
            else:
                nc.vector.tensor_tensor(factor[:], top[:], root[:], ALU.mult)
                nc.vector.tensor_tensor(result[:], factor[:], root[:], ALU.mult)
            nc.sync.dma_start(out_rows[:, t, lo:hi], result[:])

        out_pieces = [(t, 0, S) for t in range(PLANES - 1)] + [(PLANES - 1, lo, lo + HALF) for lo in (0, HALF)]
        fetched = [fetch(*piece) for piece in out_pieces[:LEAD]]
        for i, piece in enumerate(out_pieces):
            if i + LEAD < len(out_pieces):
                fetched.append(fetch(*out_pieces[i + LEAD]))
            divide(*piece, *fetched[i])
